import numpy as np
import ml_dtypes

BF16 = ml_dtypes.bfloat16


def bf(x):
    return np.asarray(x, np.float32).astype(BF16)


def f32(x):
    return np.asarray(x, np.float32)


def f64(x):
    return np.asarray(x).astype(np.float64)


def striped(idx):
    return np.concatenate([l.reshape(-1, 16).T for l in idx])


def rows(idx, k):
    return np.tile(np.repeat(idx, 16, axis=0), (k // (16 * 8), 1))


def look(tab, idx):
    return np.take_along_axis(f64(tab), rows(idx, len(tab)), axis=1)


K, S, V, N, M = 256, 2048, 2048, 2048, 512


def setup_inputs():
    return {"tab": f32(np.random.standard_normal((2, K, S))), "y": f32(np.random.standard_normal((K, V))), "w": bf(np.random.standard_normal((K, M)) / np.sqrt(K)), "b": f32(0.5 * np.random.standard_normal((M, 1))), "offs": striped(np.stack([np.random.permutation(S)[:N] for _ in range(8)]))}


def reference(tab, y, w, b, offs):
    idx = np.stack([g.T.reshape(-1) for g in np.split(offs, 8)])
    x = (np.minimum(look(tab[0], idx), f64(y))) * (1.0 / (1.0 + np.exp(-look(tab[1], idx))))
    return np.maximum(f64(w).T @ x + f64(b), 0.0)

@@ -1,0 +1,66 @@
+import concourse.mybir as mybir
+
+F32, BF16, U16 = mybir.dt.float32, mybir.dt.bfloat16, mybir.dt.uint16
+ALU = mybir.AluOpType
+ACT = mybir.ActivationFunctionType
+
+P = 128
+PIECE = 512
+FLOPS = 2 * 256 * 512 * 2048
+
+
+def tile_lookup_vg_minsig_relu_kernel(tc, tab, y, w, b, offs, out):
+    nc = tc.nc
+    rows, places = tab.shape[1], tab.shape[2]
+    n = y.shape[1]
+    blocks, pieces, groups = rows // P, n // PIECE, w.shape[1] // P
+    half = n // 2
+    out_rows = out.rearrange("(p c) n -> p c n", c=groups)
+
+    with (
+        tc.tile_pool(name="held", bufs=1) as held,
+        tc.tile_pool(name="work", bufs=1) as work,
+        tc.psum_pool(name="psum", bufs=8) as psum,
+    ):
+        offsets = held.tile([P, n // 16], U16, name="offsets")
+        values = [held.tile([P, places], F32, name=f"values{k}") for k in range(blocks)]
+        gates = [held.tile([P, places], F32, name=f"gates{k}") for k in range(blocks)]
+        stream = [held.tile([P, n], F32, name=f"stream{k}") for k in range(blocks)]
+        weights = held.tile([P, blocks, groups * P], BF16, name="weights")
+        bias = held.tile([P, groups], F32, name="bias")
+
+        nc.sync.dma_start(offsets[:], offs)
+        nc.sync.dma_start(values[0][:], tab[0, 0:P, :])
+        nc.sync.dma_start(stream[0][:, :half], y[0:P, :half])
+        nc.sync.dma_start(gates[0][:], tab[1, 0:P, :])
+        nc.sync.dma_start(stream[0][:, half:], y[0:P, half:])
+        nc.sync.dma_start(gates[1][:], tab[1, P:, :])
+        nc.sync.dma_start(weights[:], w.rearrange("(k p) m -> p k m", p=P))
+        nc.sync.dma_start(bias[:], b.rearrange("(p c) o -> p (c o)", c=groups))
+        nc.sync.dma_start(values[1][:], tab[0, P:, :])
+        nc.sync.dma_start(stream[1][:, :half], y[P:, :half])
+        nc.sync.dma_start(stream[1][:, half:], y[P:, half:])
+        weights_by_group = weights[:].rearrange("p k (m c) -> p k c m", c=groups)
+
+        for j in range(pieces):
+            columns = slice(j * PIECE, (j + 1) * PIECE)
+            entries = offsets[:, j * PIECE // 16 : (j + 1) * PIECE // 16]
+            x = []
+            for k in range(blocks):
+                capped = work.tile([P, PIECE], F32, name=f"capped{j}_{k}")
+                gate = work.tile([P, PIECE], F32, name=f"gate{j}_{k}")
+                product = work.tile([P, PIECE], BF16, name=f"product{j}_{k}")
+                nc.vector.tensor_tensor(capped[:], values[k][:].indirect(entries), stream[k][:, columns], ALU.min)
+                nc.scalar.activation(gate[:], gates[k][:].indirect(entries), ACT.Sigmoid)
+                nc.vector.tensor_tensor(product[:], capped[:], gate[:], ALU.mult)
+                x.append(product)
+            for c in range(groups):
+                acc = psum.tile([P, PIECE], F32, name="acc")
+                for k in range(blocks):
+                    nc.tensor.matmul(acc[:], weights_by_group[:, k, c, :], x[k][:], start=k == 0, stop=k == blocks - 1)
+                result = work.tile([P, PIECE], F32, name=f"result{j}_{c}")
+                if j == pieces - 1 and c % 2 == 1:
+                    nc.vector.tensor_scalar(result[:], acc[:], bias[:, c : c + 1], 0.0, ALU.add, ALU.max)
+                else:
+                    nc.scalar.activation(result[:], acc[:], ACT.Relu, bias=bias[:, c : c + 1])
+                nc.sync.dma_start(out_rows[:, c, columns], result[:])

@@ -14,7 +14,7 @@ def tile_lookup_vg_minsig_relu_kernel(tc, tab, y, w, b, offs, out):
     rows, places = tab.shape[1], tab.shape[2]
     n = y.shape[1]
     blocks, pieces, groups = rows // P, n // PIECE, w.shape[1] // P
-    half = n // 2
+    early = pieces // 2
     out_rows = out.rearrange("(p c) n -> p c n", c=groups)
 
     with (
@@ -29,17 +29,24 @@ def tile_lookup_vg_minsig_relu_kernel(tc, tab, y, w, b, offs, out):
         weights = held.tile([P, blocks, groups * P], BF16, name="weights")
         bias = held.tile([P, groups], F32, name="bias")
 
+        def load_stream(k, first, last):
+            columns = slice(first * PIECE, last * PIECE)
+            nc.sync.dma_start(stream[k][:, columns], y[k * P : (k + 1) * P, columns])
+
         nc.sync.dma_start(offsets[:], offs)
-        nc.sync.dma_start(values[0][:], tab[0, 0:P, :])
-        nc.sync.dma_start(stream[0][:, :half], y[0:P, :half])
         nc.sync.dma_start(gates[0][:], tab[1, 0:P, :])
-        nc.sync.dma_start(stream[0][:, half:], y[0:P, half:])
+        nc.sync.dma_start(values[0][:], tab[0, 0:P, :])
+        load_stream(0, 0, early)
         nc.sync.dma_start(gates[1][:], tab[1, P:, :])
-        nc.sync.dma_start(weights[:], w.rearrange("(k p) m -> p k m", p=P))
-        nc.sync.dma_start(bias[:], b.rearrange("(p c) o -> p (c o)", c=groups))
+        nc.sync.dma_start(weights[:, 0, :], w[0:P, :])
         nc.sync.dma_start(values[1][:], tab[0, P:, :])
-        nc.sync.dma_start(stream[1][:, :half], y[P:, :half])
-        nc.sync.dma_start(stream[1][:, half:], y[P:, half:])
+        load_stream(1, 0, 1)
+        nc.sync.dma_start(weights[:, 1, :], w[P:, :])
+        nc.sync.dma_start(bias[:], b.rearrange("(p c) o -> p (c o)", c=groups))
+        load_stream(1, 1, early)
+        for j in range(early, pieces):
+            for k in range(blocks):
+                load_stream(k, j, j + 1)
         weights_by_group = weights[:].rearrange("p k (m c) -> p k c m", c=groups)
 
         for j in range(pieces):

@@ -14,7 +14,7 @@ def tile_lookup_vg_minsig_relu_kernel(tc, tab, y, w, b, offs, out):
     rows, places = tab.shape[1], tab.shape[2]
     n = y.shape[1]
     blocks, pieces, groups = rows // P, n // PIECE, w.shape[1] // P
-    early = pieces // 2
+    early = pieces - 1
     out_rows = out.rearrange("(p c) n -> p c n", c=groups)
 
     with (
@@ -36,38 +36,55 @@ def tile_lookup_vg_minsig_relu_kernel(tc, tab, y, w, b, offs, out):
         nc.sync.dma_start(offsets[:], offs)
         nc.sync.dma_start(gates[0][:], tab[1, 0:P, :])
         nc.sync.dma_start(values[0][:], tab[0, 0:P, :])
-        load_stream(0, 0, early)
+        load_stream(0, 0, 1)
+        load_stream(0, 1, early)
         nc.sync.dma_start(gates[1][:], tab[1, P:, :])
         nc.sync.dma_start(weights[:, 0, :], w[0:P, :])
         nc.sync.dma_start(values[1][:], tab[0, P:, :])
         load_stream(1, 0, 1)
         nc.sync.dma_start(weights[:, 1, :], w[P:, :])
         nc.sync.dma_start(bias[:], b.rearrange("(p c) o -> p (c o)", c=groups))
-        load_stream(1, 1, early)
-        for j in range(early, pieces):
-            for k in range(blocks):
-                load_stream(k, j, j + 1)
+        load_stream(1, 1, 2)
+        load_stream(1, 2, pieces)
+        load_stream(0, early, pieces)
         weights_by_group = weights[:].rearrange("p k (m c) -> p k c m", c=groups)
 
+        warm_in = held.tile([P, 1], F32, name="warm_in")
+        warm_out = held.tile([P, 1], F32, name="warm_out")
+        nc.vector.memset(warm_in[:], 0.0)
+        nc.scalar.activation(warm_out[:], warm_in[:], ACT.Sigmoid)
+
+        def entries(j):
+            return offsets[:, j * PIECE // 16 : (j + 1) * PIECE // 16]
+
+        gate = {}
+        for k in range(blocks):
+            for j in range(pieces):
+                gate[k, j] = work.tile([P, PIECE], F32, name=f"gate{k}_{j}")
+                nc.scalar.activation(gate[k, j][:], gates[k][:].indirect(entries(j)), ACT.Sigmoid)
+
+        x = {}
+
+        def gated_values(pairs):
+            capped = {}
+            for k, j in pairs:
+                capped[k, j] = work.tile([P, PIECE], F32, name=f"capped{k}_{j}")
+                piece_of_stream = stream[k][:, j * PIECE : (j + 1) * PIECE]
+                nc.vector.tensor_tensor(capped[k, j][:], values[k][:].indirect(entries(j)), piece_of_stream, ALU.min)
+            for k, j in pairs:
+                x[k, j] = work.tile([P, PIECE], BF16, name=f"x{k}_{j}")
+                nc.vector.tensor_tensor(x[k, j][:], capped[k, j][:], gate[k, j][:], ALU.mult)
+
+        gated_values([(0, j) for j in range(early)])
         for j in range(pieces):
-            columns = slice(j * PIECE, (j + 1) * PIECE)
-            entries = offsets[:, j * PIECE // 16 : (j + 1) * PIECE // 16]
-            x = []
-            for k in range(blocks):
-                capped = work.tile([P, PIECE], F32, name=f"capped{j}_{k}")
-                gate = work.tile([P, PIECE], F32, name=f"gate{j}_{k}")
-                product = work.tile([P, PIECE], BF16, name=f"product{j}_{k}")
-                nc.vector.tensor_tensor(capped[:], values[k][:].indirect(entries), stream[k][:, columns], ALU.min)
-                nc.scalar.activation(gate[:], gates[k][:].indirect(entries), ACT.Sigmoid)
-                nc.vector.tensor_tensor(product[:], capped[:], gate[:], ALU.mult)
-                x.append(product)
+            gated_values([(1, j), (0, early)] if j == early - 1 else [(1, j)])
             for c in range(groups):
                 acc = psum.tile([P, PIECE], F32, name="acc")
                 for k in range(blocks):
-                    nc.tensor.matmul(acc[:], weights_by_group[:, k, c, :], x[k][:], start=k == 0, stop=k == blocks - 1)
+                    nc.tensor.matmul(acc[:], weights_by_group[:, k, c, :], x[k, j][:], start=k == 0, stop=k == blocks - 1)
                 result = work.tile([P, PIECE], F32, name=f"result{j}_{c}")
                 if j == pieces - 1 and c % 2 == 1:
                     nc.vector.tensor_scalar(result[:], acc[:], bias[:, c : c + 1], 0.0, ALU.add, ALU.max)
                 else:
                     nc.scalar.activation(result[:], acc[:], ACT.Relu, bias=bias[:, c : c + 1])
-                nc.sync.dma_start(out_rows[:, c, columns], result[:])
+                nc.sync.dma_start(out_rows[:, c, j * PIECE : (j + 1) * PIECE], result[:])

@@ -15,23 +15,24 @@ def tile_lookup_vg_minsig_relu_kernel(tc, tab, y, w, b, offs, out):
     n = y.shape[1]
     blocks, pieces, groups = rows // P, n // PIECE, w.shape[1] // P
     early = pieces - 1
+    y_blocks = y.rearrange("(k p) n -> p k n", p=P)
     out_rows = out.rearrange("(p c) n -> p c n", c=groups)
 
     with (
         tc.tile_pool(name="held", bufs=1) as held,
         tc.tile_pool(name="work", bufs=1) as work,
-        tc.psum_pool(name="psum", bufs=8) as psum,
+        tc.psum_pool(name="psum", bufs=1) as psum,
     ):
         offsets = held.tile([P, n // 16], U16, name="offsets")
         values = [held.tile([P, places], F32, name=f"values{k}") for k in range(blocks)]
         gates = [held.tile([P, places], F32, name=f"gates{k}") for k in range(blocks)]
-        stream = [held.tile([P, n], F32, name=f"stream{k}") for k in range(blocks)]
+        stream = held.tile([P, blocks, n], F32, name="stream")
         weights = held.tile([P, blocks, groups * P], BF16, name="weights")
         bias = held.tile([P, groups], F32, name="bias")
 
         def load_stream(k, first, last):
             columns = slice(first * PIECE, last * PIECE)
-            nc.sync.dma_start(stream[k][:, columns], y[k * P : (k + 1) * P, columns])
+            nc.sync.dma_start(stream[:, k, columns], y_blocks[:, k, columns])
 
         nc.sync.dma_start(offsets[:], offs)
         nc.sync.dma_start(gates[0][:], tab[1, 0:P, :])
@@ -44,14 +45,13 @@ def tile_lookup_vg_minsig_relu_kernel(tc, tab, y, w, b, offs, out):
         load_stream(1, 0, 1)
         nc.sync.dma_start(weights[:, 1, :], w[P:, :])
         nc.sync.dma_start(bias[:], b.rearrange("(p c) o -> p (c o)", c=groups))
-        load_stream(1, 1, 2)
-        load_stream(1, 2, pieces)
-        load_stream(0, early, pieces)
+        load_stream(1, 1, early)
+        load_stream(slice(0, blocks), early, pieces)
         weights_by_group = weights[:].rearrange("p k (m c) -> p k c m", c=groups)
 
         warm_in = held.tile([P, 1], F32, name="warm_in")
         warm_out = held.tile([P, 1], F32, name="warm_out")
-        nc.vector.memset(warm_in[:], 0.0)
+        nc.gpsimd.memset(warm_in[:], 0.0)
         nc.scalar.activation(warm_out[:], warm_in[:], ACT.Sigmoid)
 
         def entries(j):
@@ -67,24 +67,31 @@ def tile_lookup_vg_minsig_relu_kernel(tc, tab, y, w, b, offs, out):
 
         def gated_values(pairs):
             capped = {}
-            for k, j in pairs:
-                capped[k, j] = work.tile([P, PIECE], F32, name=f"capped{k}_{j}")
-                piece_of_stream = stream[k][:, j * PIECE : (j + 1) * PIECE]
-                nc.vector.tensor_tensor(capped[k, j][:], values[k][:].indirect(entries(j)), piece_of_stream, ALU.min)
-            for k, j in pairs:
+
+            def product(k, j):
                 x[k, j] = work.tile([P, PIECE], BF16, name=f"x{k}_{j}")
                 nc.vector.tensor_tensor(x[k, j][:], capped[k, j][:], gate[k, j][:], ALU.mult)
 
+            for i, (k, j) in enumerate(pairs):
+                capped[k, j] = work.tile([P, PIECE], F32, name=f"capped{k}_{j}")
+                piece_of_stream = stream[:, k, j * PIECE : (j + 1) * PIECE]
+                nc.vector.tensor_tensor(capped[k, j][:], values[k][:].indirect(entries(j)), piece_of_stream, ALU.min)
+                if i > 0:
+                    product(*pairs[i - 1])
+            product(*pairs[-1])
+
         gated_values([(0, j) for j in range(early)])
+        gated_values([(1, 0)])
+        gated_values([(1, j) for j in range(1, early)] + [(k, early) for k in range(blocks)])
         for j in range(pieces):
-            gated_values([(1, j), (0, early)] if j == early - 1 else [(1, j)])
+            acc = [psum.tile([P, PIECE], F32, name=f"acc{j % 2}_{c}") for c in range(groups)]
             for c in range(groups):
-                acc = psum.tile([P, PIECE], F32, name="acc")
                 for k in range(blocks):
-                    nc.tensor.matmul(acc[:], weights_by_group[:, k, c, :], x[k, j][:], start=k == 0, stop=k == blocks - 1)
+                    nc.tensor.matmul(acc[c][:], weights_by_group[:, k, c, :], x[k, j][:], start=k == 0, stop=k == blocks - 1)
+            for c in range(groups):
                 result = work.tile([P, PIECE], F32, name=f"result{j}_{c}")
                 if j == pieces - 1 and c % 2 == 1:
-                    nc.vector.tensor_scalar(result[:], acc[:], bias[:, c : c + 1], 0.0, ALU.add, ALU.max)
+                    nc.vector.tensor_scalar(result[:], acc[c][:], bias[:, c : c + 1], 0.0, ALU.add, ALU.max)
                 else:
-                    nc.scalar.activation(result[:], acc[:], ACT.Relu, bias=bias[:, c : c + 1])
+                    nc.scalar.activation(result[:], acc[c][:], ACT.Relu, bias=bias[:, c : c + 1])
                 nc.sync.dma_start(out_rows[:, c, j * PIECE : (j + 1) * PIECE], result[:])

@@ -44,15 +44,10 @@ def tile_lookup_vg_minsig_relu_kernel(tc, tab, y, w, b, offs, out):
         nc.sync.dma_start(values[1][:], tab[0, P:, :])
         load_stream(1, 0, 1)
         nc.sync.dma_start(weights[:, 1, :], w[P:, :])
-        nc.sync.dma_start(bias[:], b.rearrange("(p c) o -> p (c o)", c=groups))
         load_stream(1, 1, early)
+        nc.sync.dma_start(bias[:], b.rearrange("(p c) o -> p (c o)", c=groups))
         load_stream(slice(0, blocks), early, pieces)
         weights_by_group = weights[:].rearrange("p k (m c) -> p k c m", c=groups)
-
-        warm_in = held.tile([P, 1], F32, name="warm_in")
-        warm_out = held.tile([P, 1], F32, name="warm_out")
-        nc.gpsimd.memset(warm_in[:], 0.0)
-        nc.scalar.activation(warm_out[:], warm_in[:], ACT.Sigmoid)
 
         def entries(j):
             return offsets[:, j * PIECE // 16 : (j + 1) * PIECE // 16]

import concourse.mybir as mybir

F32, BF16, U16 = mybir.dt.float32, mybir.dt.bfloat16, mybir.dt.uint16
ALU = mybir.AluOpType
ACT = mybir.ActivationFunctionType

P = 128
PIECE = 512
FLOPS = 2 * 256 * 512 * 2048


def tile_lookup_vg_minsig_relu_kernel(tc, tab, y, w, b, offs, out):
    nc = tc.nc
    rows, places = tab.shape[1], tab.shape[2]
    n = y.shape[1]
    blocks, pieces, groups = rows // P, n // PIECE, w.shape[1] // P
    early = pieces - 1
    y_blocks = y.rearrange("(k p) n -> p k n", p=P)
    out_rows = out.rearrange("(p c) n -> p c n", c=groups)

    with (
        tc.tile_pool(name="held", bufs=1) as held,
        tc.tile_pool(name="work", bufs=1) as work,
        tc.psum_pool(name="psum", bufs=1) as psum,
    ):
        offsets = held.tile([P, n // 16], U16, name="offsets")
        values = [held.tile([P, places], F32, name=f"values{k}") for k in range(blocks)]
        gates = [held.tile([P, places], F32, name=f"gates{k}") for k in range(blocks)]
        stream = held.tile([P, blocks, n], F32, name="stream")
        weights = held.tile([P, blocks, groups * P], BF16, name="weights")
        bias = held.tile([P, groups], F32, name="bias")

        def load_stream(k, first, last):
            columns = slice(first * PIECE, last * PIECE)
            nc.sync.dma_start(stream[:, k, columns], y_blocks[:, k, columns])

        nc.sync.dma_start(offsets[:], offs)
        nc.sync.dma_start(gates[0][:], tab[1, 0:P, :])
        nc.sync.dma_start(values[0][:], tab[0, 0:P, :])
        load_stream(0, 0, 1)
        load_stream(0, 1, early)
        nc.sync.dma_start(gates[1][:], tab[1, P:, :])
        nc.sync.dma_start(weights[:, 0, :], w[0:P, :])
        nc.sync.dma_start(values[1][:], tab[0, P:, :])
        load_stream(1, 0, 1)
        nc.sync.dma_start(weights[:, 1, :], w[P:, :])
        load_stream(1, 1, early)
        nc.sync.dma_start(bias[:], b.rearrange("(p c) o -> p (c o)", c=groups))
        load_stream(slice(0, blocks), early, pieces)
        weights_by_group = weights[:].rearrange("p k (m c) -> p k c m", c=groups)

        def entries(j):
            return offsets[:, j * PIECE // 16 : (j + 1) * PIECE // 16]

        gate = {}
        for k in range(blocks):
            for j in range(pieces):
                gate[k, j] = work.tile([P, PIECE], F32, name=f"gate{k}_{j}")
                nc.scalar.activation(gate[k, j][:], gates[k][:].indirect(entries(j)), ACT.Sigmoid)

        x = {}

        def gated_values(pairs):
            capped = {}

            def product(k, j):
                x[k, j] = work.tile([P, PIECE], BF16, name=f"x{k}_{j}")
                nc.vector.tensor_tensor(x[k, j][:], capped[k, j][:], gate[k, j][:], ALU.mult)

            for i, (k, j) in enumerate(pairs):
                capped[k, j] = work.tile([P, PIECE], F32, name=f"capped{k}_{j}")
                piece_of_stream = stream[:, k, j * PIECE : (j + 1) * PIECE]
                nc.vector.tensor_tensor(capped[k, j][:], values[k][:].indirect(entries(j)), piece_of_stream, ALU.min)
                if i > 0:
                    product(*pairs[i - 1])
            product(*pairs[-1])

        gated_values([(0, j) for j in range(early)])
        gated_values([(1, 0)])
        gated_values([(1, j) for j in range(1, early)] + [(k, early) for k in range(blocks)])
        for j in range(pieces):
            acc = [psum.tile([P, PIECE], F32, name=f"acc{j % 2}_{c}") for c in range(groups)]
            for c in range(groups):
                for k in range(blocks):
                    nc.tensor.matmul(acc[c][:], weights_by_group[:, k, c, :], x[k, j][:], start=k == 0, stop=k == blocks - 1)
            for c in range(groups):
                result = work.tile([P, PIECE], F32, name=f"result{j}_{c}")
                if j == pieces - 1 and c % 2 == 1:
                    nc.vector.tensor_scalar(result[:], acc[c][:], bias[:, c : c + 1], 0.0, ALU.add, ALU.max)
                else:
                    nc.scalar.activation(result[:], acc[c][:], ACT.Relu, bias=bias[:, c : c + 1])
                nc.sync.dma_start(out_rows[:, c, j * PIECE : (j + 1) * PIECE], result[:])
